import numpy as np
import ml_dtypes


def mxq(x, axis, fmt="e4m3"):
    dtype, down = {"e4m3": (ml_dtypes.float8_e4m3fn, 7), "e5m2": (ml_dtypes.float8_e5m2, 14)}[fmt]
    v = np.moveaxis(np.asarray(x, np.float32).astype(ml_dtypes.bfloat16).astype(np.float64), axis, -1)
    blocks = v.reshape(v.shape[:-1] + (-1, 32))
    amax = np.abs(blocks).max(-1, keepdims=True)
    byte = np.maximum(np.where(amax > 0, np.frexp(amax)[1] - 1 + 127, 0) - down, 1)
    scale = np.exp2(byte - 127.0)
    codes = (blocks / scale).astype(np.float32).astype(dtype).astype(np.float64)
    return np.moveaxis((codes * scale).reshape(v.shape), -1, axis)


WIDE = False


def mx_kscale(k):
    if not WIDE:
        return np.ones(k)
    levels = np.array([10, -10, 5, -5, 0])
    if k % 512:
        return np.exp2(np.random.permutation(np.resize(levels, k // 32))).repeat(32)
    a = np.empty((k // 512, 16))
    for p in range(k // 512):
        a[p, :8] = np.random.permutation(np.resize(levels, 8))
        for g in range(8):
            far = levels[np.abs(levels - a[p, g]) >= 10]
            a[p, g + 8] = far[np.random.randint(len(far))]
    return np.exp2(a.ravel()).repeat(32)


def f64(x):
    return np.asarray(x).astype(np.float64)


def striped(idx):
    return np.tile(idx.reshape(-1, 16).T, (8, 1)).astype(np.uint16)


def unstriped(offs):
    return offs[:16].T.reshape(-1).astype(np.int64)


def relu(v):
    return np.maximum(v, 0.0)


K, T, E, C, H, N = 512, 1024, 8, 256, 512, 256


def by_expert(wq, xq):
    return np.concatenate([wq[e].T @ xq[:, e * C:(e + 1) * C] for e in range(E)], axis=1)


def setup_inputs():
    n = np.random.standard_normal
    s = mx_kscale(K)[:, None]
    u = mx_kscale(H)
    first = np.random.permutation(np.repeat(np.arange(E), T // E))
    second = (first + 1 + np.random.permutation(np.repeat(np.arange(E - 1), -(-T // (E - 1)))[:T])) % E
    while np.bincount(second, minlength=E).max() != T // E:
        load = np.bincount(second, minlength=E); hi, lo = int(load.argmax()), int(load.argmin())
        t = np.flatnonzero((second == hi) & (first != lo))[0]; second[t] = lo
    slot_token = np.empty(E * C, np.int64); pos = np.empty((2, T), np.int64); fill = np.zeros(E, np.int64)
    place = np.stack([np.random.permutation(C) for _ in range(E)])
    for r, deal in enumerate((first, second)):
        for t in np.random.permutation(T):
            e = deal[t]; j = e * C + place[e, fill[e]]; fill[e] += 1; slot_token[j] = t; pos[r, t] = j
    g = np.random.uniform(0.2, 0.8, T)
    return {
        "xT": (n((K, T)) * s).astype(np.float32),
        "w1": (n((E, K, H)) / np.sqrt(K) / s[None] * u[None, None, :]).astype(np.float32),
        "w2": (n((E, H, N)) / np.sqrt(H) / u[None, :, None]).astype(np.float32),
        "gate": np.stack([np.tile(g, (N, 1)), np.tile(1.0 - g, (N, 1))]).astype(np.float32),
        "offs": striped(slot_token),
        "pos1": striped(pos[0]),
        "pos2": striped(pos[1]),
    }


def reference(xT, w1, w2, gate, offs, pos1, pos2):
    idx = unstriped(offs)
    xq = mxq(f64(xT)[:, idx], 0, "e4m3")
    h = relu(by_expert(mxq(f64(w1), 1, "e4m3"), xq))
    y = by_expert(mxq(f64(w2), 1, "e4m3"), mxq(h, 0, "e4m3"))
    return f64(gate[0]) * y[:, unstriped(pos1)] + f64(gate[1]) * y[:, unstriped(pos2)]

@@ -1,0 +1,168 @@
+from contextlib import ExitStack
+
+import concourse.mybir as mybir
+
+K, T, E, C, H, N = 512, 1024, 8, 256, 512, 256
+FLOPS = 2 * E * C * (K * H + H * N)
+
+F32 = mybir.dt.float32
+BF16 = mybir.dt.bfloat16
+U32 = mybir.dt.uint32
+U16 = mybir.dt.uint16
+U8 = mybir.dt.uint8
+FP8X4 = mybir.dt.float8_e4m3fn_x4
+MULT = mybir.AluOpType.mult
+RELU = mybir.ActivationFunctionType.Relu
+
+P = 128
+X_CHUNKS = ((0, 256), (256, 512), (512, 1024))
+X_VECTOR = (0, 256, 256)
+W1_VECTOR = (64, 0, 128, 0, 0, 128, 0, 64)
+W2_VECTOR = (256, 256, 0, 256, 256, 0, 256, 128)
+PAIR = 512
+HALF = 128
+
+
+def tile_routed_moe_kernel(tc, xT, w1, w2, gate, offs, pos1, pos2, out):
+    nc = tc.nc
+    with ExitStack() as ctx:
+        keep = ctx.enter_context(tc.tile_pool(name="keep", bufs=1))
+        raws = ctx.enter_context(tc.tile_pool(name="raws", bufs=1))
+        work = ctx.enter_context(tc.tile_pool(name="work", bufs=3))
+        codes = ctx.enter_context(tc.tile_pool(name="codes", bufs=4))
+        psum = ctx.enter_context(tc.psum_pool(name="psum", bufs=4))
+
+        offs_sb = keep.tile([P, E * C // 16], U16, name="offs_sb")
+        pos1_sb = keep.tile([P, T // 16], U16, name="pos1_sb")
+        pos2_sb = keep.tile([P, T // 16], U16, name="pos2_sb")
+        x_codes = keep.tile([P, T], U32, name="x_codes", align_bytes=64)
+        x_scales = keep.tile([P, T], U8, name="x_scales", align_bytes=64)
+        y_sb = [keep.tile([P, E * C], F32, name=f"y_sb{b}") for b in range(2)]
+
+        nc.sync.dma_start(offs_sb[:], offs)
+        x_view = xT.rearrange("(p j) n -> p j n", j=4)
+        x_raw = []
+        for i, (t0, t1) in enumerate(X_CHUNKS):
+            r = raws.tile([P, 4, t1 - t0], F32, name=f"x_raw{i}")
+            nc.sync.dma_start(r[:], x_view[:, :, t0:t1])
+            x_raw.append(r)
+        w1_raw, w2_raw = {}, {}
+        order = [("1", 0), ("1", 1), ("1", 2), ("1", 3), ("2", 0), ("1", 4), ("2", 1), ("1", 5), ("2", 2),
+                 ("1", 6), ("2", 3), ("1", 7), ("2", 4), ("2", 5), ("2", 6), ("2", 7)]
+        for which, e in order:
+            if which == "1":
+                w1_raw[e] = raws.tile([P, 4, H], F32, name=f"w1_raw{e}")
+                nc.sync.dma_start(w1_raw[e][:], w1[e].rearrange("(p j) c -> p j c", j=4))
+            else:
+                w2_raw[e] = raws.tile([P, 4, N], F32, name=f"w2_raw{e}")
+                nc.sync.dma_start(w2_raw[e][:], w2[e].rearrange("(p j) c -> p j c", j=4))
+        nc.sync.dma_start(pos1_sb[:], pos1)
+        nc.sync.dma_start(pos2_sb[:], pos2)
+        gates = {}
+        for b in range(2):
+            for r in range(2):
+                g = raws.tile([P, T], F32, name=f"gate{b}{r}")
+                nc.sync.dma_start(g[:], gate[r, b * P:(b + 1) * P, :])
+                gates[b, r] = g
+
+        warm = keep.tile([P, 1], F32, name="warm")
+        nc.vector.memset(warm[:], 0.0)
+        nc.scalar.activation(warm[:], warm[:], RELU)
+        nc.gpsimd.memset(x_scales[:], 0)
+
+        def shared_copy(dst, src, count, cut):
+            if cut > 0:
+                nc.vector.tensor_copy(dst[:, :cut], src[:, :cut])
+            if cut < count:
+                nc.scalar.copy(dst[:, cut:], src[:, cut:])
+
+        def interleave(grouped, raw, width, cut):
+            dst = grouped[:].rearrange("p (c i t) -> p c t i", i=4, t=4)
+            src = raw[:].rearrange("p t (c i) -> p c t i", i=4)
+            shared_copy(dst, src, width // 4, cut // 4)
+
+        def quantize(code, scale, grouped):
+            nc.vector.quantize_mx(out=code.bitcast(FP8X4), scales=scale, in_=grouped)
+
+        for i, (t0, t1) in enumerate(X_CHUNKS):
+            xg = work.tile([P, 4 * (t1 - t0)], BF16, name="x_grouped", bufs=2, align_bytes=64)
+            interleave(xg, x_raw[i], t1 - t0, X_VECTOR[i])
+            quantize(x_codes[:, t0:t1], x_scales[:, t0:t1], xg[:])
+
+        slots = {}
+
+        def gather(pair):
+            g = codes.tile([P, PAIR], U32, name="slot_codes", bufs=3, align_bytes=64)
+            s = codes.tile([P, PAIR], U8, name="slot_scales", bufs=3, align_bytes=64)
+            o = offs_sb[:, pair * (PAIR // 16):(pair + 1) * (PAIR // 16)]
+            nc.vector.tensor_copy(g[:], x_codes[:].indirect(o))
+            nc.vector.tensor_copy(s[:], x_scales[:].indirect(o))
+            slots[pair] = (g, s)
+
+        hidden = {}
+
+        def first_layer(e):
+            if e % 2 == 0:
+                gather(e // 2)
+            g, s = slots[e // 2]
+            wg = work.tile([P, 4 * H], BF16, name="w1_grouped", bufs=4, align_bytes=64)
+            dst = wg[:].rearrange("p (t m j) -> p m j t", t=4, j=4)
+            src = w1_raw[e][:].rearrange("p j (m t) -> p m j t", t=4)
+            shared_copy(dst, src, P, W1_VECTOR[e])
+            wc = codes.tile([P, H], U32, name="w1_codes", align_bytes=64)
+            ws = codes.tile([P, H], U8, name="w1_scales", align_bytes=64)
+            quantize(wc[:], ws[:], wg[:])
+            hg = work.tile([P, 4 * C], BF16, name="h_grouped", align_bytes=64)
+            for half in range(2):
+                cols = slice((e % 2) * C + half * HALF, (e % 2) * C + (half + 1) * HALF)
+                bank = psum.tile([P, 4, HALF], F32, name="h_bank")
+                for t in range(4):
+                    nc.tensor.matmul_mx(
+                        out=bank[:, t, :],
+                        lhsT=wc[:, t * P:(t + 1) * P].bitcast(FP8X4), lhsT_scale=ws[:, t * P:(t + 1) * P],
+                        rhs=g[:, cols].bitcast(FP8X4), rhs_scale=s[:, cols],
+                        start=True, stop=True,
+                    )
+                nc.scalar.activation(
+                    hg[:, half * 4 * HALF:(half + 1) * 4 * HALF].rearrange("p (n t) -> p n t", t=4),
+                    bank[:].rearrange("p t n -> p n t"), RELU)
+            hc = codes.tile([P, C], U32, name="h_codes", align_bytes=64)
+            hs = codes.tile([P, C], U8, name="h_scales", align_bytes=64)
+            quantize(hc[:], hs[:], hg[:])
+            hidden[e] = (hc, hs)
+
+        y_banks = {}
+
+        def second_layer(e):
+            wg = work.tile([P, 4 * N], BF16, name="w2_grouped", align_bytes=64)
+            interleave(wg, w2_raw[e], N, W2_VECTOR[e])
+            wc = codes.tile([P, N], U32, name="w2_codes", align_bytes=64)
+            ws = codes.tile([P, N], U8, name="w2_scales", align_bytes=64)
+            quantize(wc[:], ws[:], wg[:])
+            hc, hs = hidden[e]
+            for b in range(2):
+                if e % 2 == 0:
+                    y_banks[b] = psum.tile([P, PAIR], F32, name="y_bank")
+                nc.tensor.matmul_mx(
+                    out=y_banks[b][:, (e % 2) * C:(e % 2 + 1) * C],
+                    lhsT=wc[:, b * P:(b + 1) * P].bitcast(FP8X4), lhsT_scale=ws[:, b * P:(b + 1) * P],
+                    rhs=hc[:].bitcast(FP8X4), rhs_scale=hs[:],
+                    start=True, stop=True,
+                )
+                if e % 2 == 1:
+                    nc.scalar.copy(y_sb[b][:, (e - 1) * C:(e + 1) * C], y_banks[b][:])
+
+        for which, e in order:
+            if which == "1":
+                first_layer(e)
+            else:
+                second_layer(e)
+
+        for b, pieces in enumerate((((0, 1024),), ((0, 512), (512, 1024)))):
+            for c0, c1 in pieces:
+                p1 = work.tile([P, c1 - c0], F32, name="prod1", bufs=2)
+                p2 = work.tile([P, c1 - c0], F32, name="prod2", bufs=2)
+                nc.vector.tensor_tensor(p1[:], y_sb[b][:].indirect(pos1_sb[:, c0 // 16:c1 // 16]), gates[b, 0][:, c0:c1], MULT)
+                nc.vector.tensor_tensor(p2[:], y_sb[b][:].indirect(pos2_sb[:, c0 // 16:c1 // 16]), gates[b, 1][:, c0:c1], MULT)
+                nc.vector.tensor_add(p1[:], p1[:], p2[:])
+                nc.sync.dma_start(out[b * P:(b + 1) * P, c0:c1], p1[:])

@@ -15,10 +15,9 @@ MULT = mybir.AluOpType.mult
 RELU = mybir.ActivationFunctionType.Relu
 
 P = 128
-X_CHUNKS = ((0, 256), (256, 512), (512, 1024))
-X_VECTOR = (0, 256, 256)
-W1_VECTOR = (64, 0, 128, 0, 0, 128, 0, 64)
-W2_VECTOR = (256, 256, 0, 256, 256, 0, 256, 128)
+X_CHUNKS = ((0, 512), (512, 768), (768, 1024))
+X_VECTOR = (256, 128, 128)
+W1_VECTOR = 32
 PAIR = 512
 HALF = 128
 
@@ -106,9 +105,9 @@ def tile_routed_moe_kernel(tc, xT, w1, w2, gate, offs, pos1, pos2, out):
                 gather(e // 2)
             g, s = slots[e // 2]
             wg = work.tile([P, 4 * H], BF16, name="w1_grouped", bufs=4, align_bytes=64)
-            dst = wg[:].rearrange("p (t m j) -> p m j t", t=4, j=4)
-            src = w1_raw[e][:].rearrange("p j (m t) -> p m j t", t=4)
-            shared_copy(dst, src, P, W1_VECTOR[e])
+            dst = wg[:].rearrange("p (t m j) -> p m t j", t=4, j=4)
+            src = w1_raw[e][:].rearrange("p j (m t) -> p m t j", t=4)
+            shared_copy(dst, src, P, W1_VECTOR)
             wc = codes.tile([P, H], U32, name="w1_codes", align_bytes=64)
             ws = codes.tile([P, H], U8, name="w1_scales", align_bytes=64)
             quantize(wc[:], ws[:], wg[:])
@@ -135,21 +134,26 @@ def tile_routed_moe_kernel(tc, xT, w1, w2, gate, offs, pos1, pos2, out):
 
         def second_layer(e):
             wg = work.tile([P, 4 * N], BF16, name="w2_grouped", align_bytes=64)
-            interleave(wg, w2_raw[e], N, W2_VECTOR[e])
+            interleave(wg, w2_raw[e], N, N)
             wc = codes.tile([P, N], U32, name="w2_codes", align_bytes=64)
             ws = codes.tile([P, N], U8, name="w2_scales", align_bytes=64)
             quantize(wc[:], ws[:], wg[:])
             hc, hs = hidden[e]
+            last = e >= E - 2
             for b in range(2):
-                if e % 2 == 0:
+                if last or e % 2 == 0:
                     y_banks[b] = psum.tile([P, PAIR], F32, name="y_bank")
+                place = 0 if last else (e % 2) * C
                 nc.tensor.matmul_mx(
-                    out=y_banks[b][:, (e % 2) * C:(e % 2 + 1) * C],
+                    out=y_banks[b][:, place:place + C],
                     lhsT=wc[:, b * P:(b + 1) * P].bitcast(FP8X4), lhsT_scale=ws[:, b * P:(b + 1) * P],
                     rhs=hc[:].bitcast(FP8X4), rhs_scale=hs[:],
                     start=True, stop=True,
                 )
-                if e % 2 == 1:
+                if last:
+                    engine_copy = nc.vector.tensor_copy if (e == E - 1 and b == 0) else nc.scalar.copy
+                    engine_copy(y_sb[b][:, e * C:(e + 1) * C], y_banks[b][:, :C])
+                elif e % 2 == 1:
                     nc.scalar.copy(y_sb[b][:, (e - 1) * C:(e + 1) * C], y_banks[b][:])
 
         for which, e in order:

@@ -19,6 +19,8 @@ X_CHUNKS = ((0, 512), (512, 768), (768, 1024))
 X_VECTOR = (256, 128, 128)
 W1_VECTOR = 32
 PAIR = 512
+LOADS = (("1", 0, 1), ("1", 1, 1), ("1", 2, 2), ("2", 0, 2), ("1", 4, 2), ("2", 2, 2), ("1", 6, 2), ("2", 4, 2), ("2", 6, 1), ("2", 7, 1))
+STEPS = [(which, e0 + i) for which, e0, n in LOADS for i in range(n)]
 HALF = 128
 
 
@@ -46,15 +48,12 @@ def tile_routed_moe_kernel(tc, xT, w1, w2, gate, offs, pos1, pos2, out):
             nc.sync.dma_start(r[:], x_view[:, :, t0:t1])
             x_raw.append(r)
         w1_raw, w2_raw = {}, {}
-        order = [("1", 0), ("1", 1), ("1", 2), ("1", 3), ("2", 0), ("1", 4), ("2", 1), ("1", 5), ("2", 2),
-                 ("1", 6), ("2", 3), ("1", 7), ("2", 4), ("2", 5), ("2", 6), ("2", 7)]
-        for which, e in order:
-            if which == "1":
-                w1_raw[e] = raws.tile([P, 4, H], F32, name=f"w1_raw{e}")
-                nc.sync.dma_start(w1_raw[e][:], w1[e].rearrange("(p j) c -> p j c", j=4))
-            else:
-                w2_raw[e] = raws.tile([P, 4, N], F32, name=f"w2_raw{e}")
-                nc.sync.dma_start(w2_raw[e][:], w2[e].rearrange("(p j) c -> p j c", j=4))
+        for which, e0, n in LOADS:
+            source, width = (w1, H) if which == "1" else (w2, N)
+            r = raws.tile([P, n, 4, width], F32, name=f"w{which}_raw{e0}")
+            nc.sync.dma_start(r[:], source[e0:e0 + n].rearrange("e (p j) c -> p e j c", j=4))
+            for i in range(n):
+                (w1_raw if which == "1" else w2_raw)[e0 + i] = r[:, i]
         nc.sync.dma_start(pos1_sb[:], pos1)
         nc.sync.dma_start(pos2_sb[:], pos2)
         gates = {}
@@ -77,7 +76,7 @@ def tile_routed_moe_kernel(tc, xT, w1, w2, gate, offs, pos1, pos2, out):
 
         def interleave(grouped, raw, width, cut):
             dst = grouped[:].rearrange("p (c i t) -> p c t i", i=4, t=4)
-            src = raw[:].rearrange("p t (c i) -> p c t i", i=4)
+            src = raw.rearrange("p t (c i) -> p c t i", i=4)
             shared_copy(dst, src, width // 4, cut // 4)
 
         def quantize(code, scale, grouped):
@@ -85,14 +84,14 @@ def tile_routed_moe_kernel(tc, xT, w1, w2, gate, offs, pos1, pos2, out):
 
         for i, (t0, t1) in enumerate(X_CHUNKS):
             xg = work.tile([P, 4 * (t1 - t0)], BF16, name="x_grouped", bufs=2, align_bytes=64)
-            interleave(xg, x_raw[i], t1 - t0, X_VECTOR[i])
+            interleave(xg, x_raw[i][:], t1 - t0, X_VECTOR[i])
             quantize(x_codes[:, t0:t1], x_scales[:, t0:t1], xg[:])
 
         slots = {}
 
         def gather(pair):
-            g = codes.tile([P, PAIR], U32, name="slot_codes", bufs=3, align_bytes=64)
-            s = codes.tile([P, PAIR], U8, name="slot_scales", bufs=3, align_bytes=64)
+            g = codes.tile([P, PAIR], U32, name="slot_codes", bufs=1, align_bytes=64)
+            s = codes.tile([P, PAIR], U8, name="slot_scales", bufs=1, align_bytes=64)
             o = offs_sb[:, pair * (PAIR // 16):(pair + 1) * (PAIR // 16)]
             nc.vector.tensor_copy(g[:], x_codes[:].indirect(o))
             nc.vector.tensor_copy(s[:], x_scales[:].indirect(o))
@@ -106,7 +105,7 @@ def tile_routed_moe_kernel(tc, xT, w1, w2, gate, offs, pos1, pos2, out):
             g, s = slots[e // 2]
             wg = work.tile([P, 4 * H], BF16, name="w1_grouped", bufs=4, align_bytes=64)
             dst = wg[:].rearrange("p (t m j) -> p m t j", t=4, j=4)
-            src = w1_raw[e][:].rearrange("p j (m t) -> p m t j", t=4)
+            src = w1_raw[e].rearrange("p j (m t) -> p m t j", t=4)
             shared_copy(dst, src, P, W1_VECTOR)
             wc = codes.tile([P, H], U32, name="w1_codes", align_bytes=64)
             ws = codes.tile([P, H], U8, name="w1_scales", align_bytes=64)
@@ -156,7 +155,7 @@ def tile_routed_moe_kernel(tc, xT, w1, w2, gate, offs, pos1, pos2, out):
                 elif e % 2 == 1:
                     nc.scalar.copy(y_sb[b][:, (e - 1) * C:(e + 1) * C], y_banks[b][:])
 
-        for which, e in order:
+        for which, e in STEPS:
             if which == "1":
                 first_layer(e)
             else:

@@ -104,8 +104,8 @@ def tile_routed_moe_kernel(tc, xT, w1, w2, gate, offs, pos1, pos2, out):
                 gather(e // 2)
             g, s = slots[e // 2]
             wg = work.tile([P, 4 * H], BF16, name="w1_grouped", bufs=4, align_bytes=64)
-            dst = wg[:].rearrange("p (t m j) -> p m t j", t=4, j=4)
-            src = w1_raw[e].rearrange("p j (m t) -> p m t j", t=4)
+            dst = wg[:].rearrange("p (t m j) -> p m j t", t=4, j=4)
+            src = w1_raw[e].rearrange("p j (m t) -> p m j t", t=4)
             shared_copy(dst, src, P, W1_VECTOR)
             wc = codes.tile([P, H], U32, name="w1_codes", align_bytes=64)
             ws = codes.tile([P, H], U8, name="w1_scales", align_bytes=64)

from contextlib import ExitStack

import concourse.mybir as mybir

K, T, E, C, H, N = 512, 1024, 8, 256, 512, 256
FLOPS = 2 * E * C * (K * H + H * N)

F32 = mybir.dt.float32
BF16 = mybir.dt.bfloat16
U32 = mybir.dt.uint32
U16 = mybir.dt.uint16
U8 = mybir.dt.uint8
FP8X4 = mybir.dt.float8_e4m3fn_x4
MULT = mybir.AluOpType.mult
RELU = mybir.ActivationFunctionType.Relu

P = 128
X_CHUNKS = ((0, 512), (512, 768), (768, 1024))
X_VECTOR = (256, 128, 128)
W1_VECTOR = 32
PAIR = 512
LOADS = (("1", 0, 1), ("1", 1, 1), ("1", 2, 2), ("2", 0, 2), ("1", 4, 2), ("2", 2, 2), ("1", 6, 2), ("2", 4, 2), ("2", 6, 1), ("2", 7, 1))
STEPS = [(which, e0 + i) for which, e0, n in LOADS for i in range(n)]
HALF = 128


def tile_routed_moe_kernel(tc, xT, w1, w2, gate, offs, pos1, pos2, out):
    nc = tc.nc
    with ExitStack() as ctx:
        keep = ctx.enter_context(tc.tile_pool(name="keep", bufs=1))
        raws = ctx.enter_context(tc.tile_pool(name="raws", bufs=1))
        work = ctx.enter_context(tc.tile_pool(name="work", bufs=3))
        codes = ctx.enter_context(tc.tile_pool(name="codes", bufs=4))
        psum = ctx.enter_context(tc.psum_pool(name="psum", bufs=4))

        offs_sb = keep.tile([P, E * C // 16], U16, name="offs_sb")
        pos1_sb = keep.tile([P, T // 16], U16, name="pos1_sb")
        pos2_sb = keep.tile([P, T // 16], U16, name="pos2_sb")
        x_codes = keep.tile([P, T], U32, name="x_codes", align_bytes=64)
        x_scales = keep.tile([P, T], U8, name="x_scales", align_bytes=64)
        y_sb = [keep.tile([P, E * C], F32, name=f"y_sb{b}") for b in range(2)]

        nc.sync.dma_start(offs_sb[:], offs)
        x_view = xT.rearrange("(p j) n -> p j n", j=4)
        x_raw = []
        for i, (t0, t1) in enumerate(X_CHUNKS):
            r = raws.tile([P, 4, t1 - t0], F32, name=f"x_raw{i}")
            nc.sync.dma_start(r[:], x_view[:, :, t0:t1])
            x_raw.append(r)
        w1_raw, w2_raw = {}, {}
        for which, e0, n in LOADS:
            source, width = (w1, H) if which == "1" else (w2, N)
            r = raws.tile([P, n, 4, width], F32, name=f"w{which}_raw{e0}")
            nc.sync.dma_start(r[:], source[e0:e0 + n].rearrange("e (p j) c -> p e j c", j=4))
            for i in range(n):
                (w1_raw if which == "1" else w2_raw)[e0 + i] = r[:, i]
        nc.sync.dma_start(pos1_sb[:], pos1)
        nc.sync.dma_start(pos2_sb[:], pos2)
        gates = {}
        for b in range(2):
            for r in range(2):
                g = raws.tile([P, T], F32, name=f"gate{b}{r}")
                nc.sync.dma_start(g[:], gate[r, b * P:(b + 1) * P, :])
                gates[b, r] = g

        warm = keep.tile([P, 1], F32, name="warm")
        nc.vector.memset(warm[:], 0.0)
        nc.scalar.activation(warm[:], warm[:], RELU)
        nc.gpsimd.memset(x_scales[:], 0)

        def shared_copy(dst, src, count, cut):
            if cut > 0:
                nc.vector.tensor_copy(dst[:, :cut], src[:, :cut])
            if cut < count:
                nc.scalar.copy(dst[:, cut:], src[:, cut:])

        def interleave(grouped, raw, width, cut):
            dst = grouped[:].rearrange("p (c i t) -> p c t i", i=4, t=4)
            src = raw.rearrange("p t (c i) -> p c t i", i=4)
            shared_copy(dst, src, width // 4, cut // 4)

        def quantize(code, scale, grouped):
            nc.vector.quantize_mx(out=code.bitcast(FP8X4), scales=scale, in_=grouped)

        for i, (t0, t1) in enumerate(X_CHUNKS):
            xg = work.tile([P, 4 * (t1 - t0)], BF16, name="x_grouped", bufs=2, align_bytes=64)
            interleave(xg, x_raw[i][:], t1 - t0, X_VECTOR[i])
            quantize(x_codes[:, t0:t1], x_scales[:, t0:t1], xg[:])

        slots = {}

        def gather(pair):
            g = codes.tile([P, PAIR], U32, name="slot_codes", bufs=1, align_bytes=64)
            s = codes.tile([P, PAIR], U8, name="slot_scales", bufs=1, align_bytes=64)
            o = offs_sb[:, pair * (PAIR // 16):(pair + 1) * (PAIR // 16)]
            nc.vector.tensor_copy(g[:], x_codes[:].indirect(o))
            nc.vector.tensor_copy(s[:], x_scales[:].indirect(o))
            slots[pair] = (g, s)

        hidden = {}

        def first_layer(e):
            if e % 2 == 0:
                gather(e // 2)
            g, s = slots[e // 2]
            wg = work.tile([P, 4 * H], BF16, name="w1_grouped", bufs=4, align_bytes=64)
            dst = wg[:].rearrange("p (t m j) -> p m j t", t=4, j=4)
            src = w1_raw[e].rearrange("p j (m t) -> p m j t", t=4)
            shared_copy(dst, src, P, W1_VECTOR)
            wc = codes.tile([P, H], U32, name="w1_codes", align_bytes=64)
            ws = codes.tile([P, H], U8, name="w1_scales", align_bytes=64)
            quantize(wc[:], ws[:], wg[:])
            hg = work.tile([P, 4 * C], BF16, name="h_grouped", align_bytes=64)
            for half in range(2):
                cols = slice((e % 2) * C + half * HALF, (e % 2) * C + (half + 1) * HALF)
                bank = psum.tile([P, 4, HALF], F32, name="h_bank")
                for t in range(4):
                    nc.tensor.matmul_mx(
                        out=bank[:, t, :],
                        lhsT=wc[:, t * P:(t + 1) * P].bitcast(FP8X4), lhsT_scale=ws[:, t * P:(t + 1) * P],
                        rhs=g[:, cols].bitcast(FP8X4), rhs_scale=s[:, cols],
                        start=True, stop=True,
                    )
                nc.scalar.activation(
                    hg[:, half * 4 * HALF:(half + 1) * 4 * HALF].rearrange("p (n t) -> p n t", t=4),
                    bank[:].rearrange("p t n -> p n t"), RELU)
            hc = codes.tile([P, C], U32, name="h_codes", align_bytes=64)
            hs = codes.tile([P, C], U8, name="h_scales", align_bytes=64)
            quantize(hc[:], hs[:], hg[:])
            hidden[e] = (hc, hs)

        y_banks = {}

        def second_layer(e):
            wg = work.tile([P, 4 * N], BF16, name="w2_grouped", align_bytes=64)
            interleave(wg, w2_raw[e], N, N)
            wc = codes.tile([P, N], U32, name="w2_codes", align_bytes=64)
            ws = codes.tile([P, N], U8, name="w2_scales", align_bytes=64)
            quantize(wc[:], ws[:], wg[:])
            hc, hs = hidden[e]
            last = e >= E - 2
            for b in range(2):
                if last or e % 2 == 0:
                    y_banks[b] = psum.tile([P, PAIR], F32, name="y_bank")
                place = 0 if last else (e % 2) * C
                nc.tensor.matmul_mx(
                    out=y_banks[b][:, place:place + C],
                    lhsT=wc[:, b * P:(b + 1) * P].bitcast(FP8X4), lhsT_scale=ws[:, b * P:(b + 1) * P],
                    rhs=hc[:].bitcast(FP8X4), rhs_scale=hs[:],
                    start=True, stop=True,
                )
                if last:
                    engine_copy = nc.vector.tensor_copy if (e == E - 1 and b == 0) else nc.scalar.copy
                    engine_copy(y_sb[b][:, e * C:(e + 1) * C], y_banks[b][:, :C])
                elif e % 2 == 1:
                    nc.scalar.copy(y_sb[b][:, (e - 1) * C:(e + 1) * C], y_banks[b][:])

        for which, e in STEPS:
            if which == "1":
                first_layer(e)
            else:
                second_layer(e)

        for b, pieces in enumerate((((0, 1024),), ((0, 512), (512, 1024)))):
            for c0, c1 in pieces:
                p1 = work.tile([P, c1 - c0], F32, name="prod1", bufs=2)
                p2 = work.tile([P, c1 - c0], F32, name="prod2", bufs=2)
                nc.vector.tensor_tensor(p1[:], y_sb[b][:].indirect(pos1_sb[:, c0 // 16:c1 // 16]), gates[b, 0][:, c0:c1], MULT)
                nc.vector.tensor_tensor(p2[:], y_sb[b][:].indirect(pos2_sb[:, c0 // 16:c1 // 16]), gates[b, 1][:, c0:c1], MULT)
                nc.vector.tensor_add(p1[:], p1[:], p2[:])
                nc.sync.dma_start(out[b * P:(b + 1) * P, c0:c1], p1[:])
